import numpy as np
import ml_dtypes


def mxq(x, axis, fmt="e4m3"):
    dtype, down = {"e4m3": (ml_dtypes.float8_e4m3fn, 7), "e5m2": (ml_dtypes.float8_e5m2, 14)}[fmt]
    v = np.moveaxis(np.asarray(x, np.float32).astype(ml_dtypes.bfloat16).astype(np.float64), axis, -1)
    blocks = v.reshape(v.shape[:-1] + (-1, 32))
    amax = np.abs(blocks).max(-1, keepdims=True)
    byte = np.maximum(np.where(amax > 0, np.frexp(amax)[1] - 1 + 127, 0) - down, 1)
    scale = np.exp2(byte - 127.0)
    codes = (blocks / scale).astype(np.float32).astype(dtype).astype(np.float64)
    return np.moveaxis((codes * scale).reshape(v.shape), -1, axis)


WIDE = False


def mx_kscale(k):
    if not WIDE:
        return np.ones(k)
    levels = np.array([10, -10, 5, -5, 0])
    if k % 512:
        return np.exp2(np.random.permutation(np.resize(levels, k // 32))).repeat(32)
    a = np.empty((k // 512, 16))
    for p in range(k // 512):
        a[p, :8] = np.random.permutation(np.resize(levels, 8))
        for g in range(8):
            far = levels[np.abs(levels - a[p, g]) >= 10]
            a[p, g + 8] = far[np.random.randint(len(far))]
    return np.exp2(a.ravel()).repeat(32)


def f64(x):
    return np.asarray(x).astype(np.float64)


def striped(idx):
    return np.tile(idx.reshape(-1, 16).T, (8, 1)).astype(np.uint16)


def unstriped(offs):
    return offs[:16].T.reshape(-1).astype(np.int64)


E2M1 = np.array([0.0, 0.5, 1.0, 1.5, 2.0, 3.0, 4.0, 6.0, -0.0, -0.5, -1.0, -1.5, -2.0, -3.0, -4.0, -6.0])


def pack_weight(w, fmt):
    k, n = w.shape
    w = f64(np.asarray(w, np.float32).astype(ml_dtypes.bfloat16)).reshape(k // 32, 32, n)
    amax = np.abs(w).max(1)
    if fmt == "e4m3":
        byte = np.frexp(amax)[1] - 1 + 127 - 7
    else:
        mant, ex = np.frexp(amax / 6.0)
        byte = np.where(mant > 0.5, ex, ex - 1) + 127
    byte = np.clip(np.where(amax > 0, byte, 1), 1, 254)
    scaled = (w * np.exp2(127.0 - byte)[:, None, :]).reshape(k, n).astype(np.float32)
    by_word = np.ascontiguousarray(scaled.reshape(k // 512, 128, 4, n).transpose(0, 1, 3, 2))
    if fmt == "e4m3":
        words = by_word.astype(ml_dtypes.float8_e4m3fn).view(np.uint8)
    else:
        c = by_word.astype(ml_dtypes.float4_e2m1fn).view(np.uint8) & 0xF
        words = (c[..., 0::2] | (c[..., 1::2] << 4)).reshape(k // 512, 128, 2 * n)
    return np.ascontiguousarray(words), np.ascontiguousarray(byte.astype(np.uint8).reshape(k // 512, 16, n))


def unpack_weight(words, scales, fmt):
    g, _, n = scales.shape
    words = np.ascontiguousarray(words).reshape(g, 128, n, -1)
    if fmt == "e4m3":
        vals = words.view(ml_dtypes.float8_e4m3fn).astype(np.float64)
    else:
        nib = np.empty((g, 128, n, 4), np.uint8)
        nib[..., 0::2] = words & 0xF
        nib[..., 1::2] = words >> 4
        vals = E2M1[nib]
    vals = vals * np.repeat(np.exp2(scales.astype(np.float64) - 127.0), 8, axis=1)[..., None]
    return vals.transpose(0, 1, 3, 2).reshape(g * 512, n)


def gelu(v):
    return 0.5 * v * (1.0 + np.tanh(np.sqrt(2.0 / np.pi) * (v + 0.044715 * v**3)))


def striped8(idx):
    return np.concatenate([v.reshape(-1, 16).T for v in idx]).astype(np.uint16)


def unstriped8(offs):
    return np.stack([offs[16 * g:16 * g + 16].T.reshape(-1) for g in range(8)]).astype(np.int64)


def put_heads(h, wgs, idx8, t2):
    r = np.arange(h.shape[0])
    page = np.zeros((h.shape[0], t2))
    page[r[:, None], idx8[r % 512 // 64]] = wgs[r // 4 % 128] * h
    return page


K, T, S, H, HU, T2, P, N = 1024, 2048, 512, 1024, 512, 1024, 512, 512

def setup_inputs():
    n = np.random.standard_normal
    s = mx_kscale(K)[:, None]
    u = mx_kscale(H)[:, None]
    tab_words, tab_scales = pack_weight(n((K, T)) * s, "e4m3")
    wa_words, wa_scales = pack_weight(n((K, H)) * 0.19 / np.sqrt(K) / s, "e2m1")
    wl_words, wl_scales = pack_weight(n((HU, N)) * 1.4 / np.sqrt(H) / u[HU:], "e2m1")
    slots = np.stack([np.random.permutation(T2)[:S] for _ in range(8)])
    return {
        "tab_words": tab_words, "tab_scales": tab_scales,
        "offs": striped(np.random.permutation(T)[:S]),
        "offs2": striped8(slots),
        "offs3": striped(np.random.permutation(T2)[:P]),
        "wa_words": wa_words, "wa_scales": wa_scales,
        "wb": (n((K, H)) * 0.19 / np.sqrt(K) / s).astype(np.float32),
        "wc": (n((K, H)) * 1.5 / np.sqrt(K) / s).astype(np.float32),
        "gt": (np.random.choice([-1.0, 1.0], H) * np.random.uniform(0.45, 0.62, H)).astype(np.float32),
        "wgs": np.repeat(np.random.uniform(0.5, 2.0, (8, S)), 16, axis=0).astype(np.float32),
        "lay": (n((H, P)) * u).astype(np.float32),
        "wu": (n((HU, N)) * 1.4 / np.sqrt(H) / u[:HU]).astype(np.float32),
        "wl_words": wl_words, "wl_scales": wl_scales,
    }

def reference(tab_words, tab_scales, offs, offs2, offs3, wa_words, wa_scales, wb, wc, gt, wgs, lay, wu, wl_words, wl_scales):
    v = unpack_weight(tab_words, tab_scales, "e4m3")[:, unstriped(offs)]
    a = unpack_weight(wa_words, wa_scales, "e2m1").T @ v
    b = mxq(f64(wb), 0, "e4m3").T @ v
    d = mxq(f64(wc), 0, "e4m3").T @ v
    h = np.maximum(a, b) + f64(gt)[:, None] * np.tanh(d)
    page = put_heads(h, f64(wgs), unstriped8(offs2), T2)
    x = page[:, unstriped(offs3)]
    z = mxq(np.cos(x) * f64(lay), 0, "e4m3")
    wlow = unpack_weight(wl_words, wl_scales, "e2m1")
    y = mxq(f64(wu), 0, "e4m3").T @ z[:HU] + wlow.T @ z[HU:]
    return 0.5 * y * (1.0 + np.tanh(np.sqrt(2.0 / np.pi) * (y + 0.044715 * y ** 3)))

@@ -1,0 +1,344 @@
+import math
+from contextlib import ExitStack
+
+import concourse.mybir as mybir
+from concourse.masks import make_identity
+
+K, T, S, H, HU, T2, M, N = 1024, 2048, 512, 1024, 512, 1024, 512, 512
+FLOPS = 2 * 3 * K * H * S + 2 * H * N * M
+
+F32 = mybir.dt.float32
+BF16 = mybir.dt.bfloat16
+I32 = mybir.dt.int32
+U32 = mybir.dt.uint32
+U16 = mybir.dt.uint16
+U8 = mybir.dt.uint8
+FP8X4 = mybir.dt.float8_e4m3fn_x4
+FP4X4 = mybir.dt.float4_e2m1fn_x4
+ALU = mybir.AluOpType
+ACT = mybir.ActivationFunctionType
+
+P = 128
+PACK = 4
+KP = P * PACK
+PASSES = K // KP
+HALVES = H // KP
+PAGES = 4
+MH = M // 2
+
+
+def tile_list_portal_tag_motion_kernel(
+    tc, tab_words, tab_scales, offs, offs2, offs3, wa_words, wa_scales, wb, wc, gt, wgs, lay, wu,
+    wl_words, wl_scales, out,
+):
+    nc = tc.nc
+    with ExitStack() as ctx:
+        keep = ctx.enter_context(tc.tile_pool(name="keep", bufs=1))
+        ring = ctx.enter_context(tc.tile_pool(name="ring", bufs=4))
+        psum = ctx.enter_context(tc.psum_pool(name="psum", bufs=2))
+
+        def held(name, shape, dtype, tag=None):
+            return keep.tile(shape, dtype, name=name, tag=tag or name, align_bytes=64)
+
+        tab_s = held("tab_s", [P, PASSES, T], U8)
+        wa_s = held("wa_s", [P, PASSES, H], U8)
+        wl_s = held("wl_s", [P, 1, N], U8)
+        nc.vector.memset(tab_s[:].bitcast(I32), 0)
+        nc.gpsimd.memset(wa_s[:].bitcast(I32), 0)
+        nc.gpsimd.memset(wl_s[:].bitcast(I32), 0)
+        pages = [held("page%d" % i, [P, T2], F32) for i in range(PAGES)]
+        for page in pages:
+            nc.vector.memset(page[:], 0.0)
+
+        ident = held("ident", [P, P], F32)
+        make_identity(nc, ident[:])
+
+        def load_scales(plane, src):
+            for q in range(4):
+                nc.sync.dma_start(
+                    out=plane[32 * q : 32 * q + 4].bitcast(I32),
+                    in_=src[:, 4 * q : 4 * q + 4, :].rearrange("a r c -> r a c").bitcast(I32),
+                )
+
+        def load_table(a):
+            words = held("tab_w%d" % a, [P, T], U32)
+            nc.sync.dma_start(
+                out=words[:].bitcast(I32), in_=tab_words[a].rearrange("p t i -> p (t i)").bitcast(I32)
+            )
+            return words
+
+        def load_list(name, src):
+            lst = keep.tile([P, S // 16], U16, name=name)
+            nc.sync.dma_start(lst[:], src)
+            return lst
+
+        def load_rows(name, src, row0, col0, width):
+            raw = held(name, [P, PACK, width], F32)
+            nc.sync.dma_start(
+                out=raw[:],
+                in_=src[row0 : row0 + KP, col0 : col0 + width].rearrange("(p j) c -> p j c", j=PACK),
+            )
+            return raw
+
+        def load_wa(b):
+            words = held("wa_w%d" % b, [P, PASSES, 2 * KP], U8)
+            nc.sync.dma_start(
+                out=words[:].bitcast(I32),
+                in_=wa_words[:, :, 2 * KP * b : 2 * KP * (b + 1)].rearrange("a p c -> p a c").bitcast(I32),
+            )
+            return words
+
+        tab_w, wa_w, wb_raw, wc_raw = {}, {}, {}, {}
+        tab_w[0] = load_table(0)
+        idx = load_list("idx", offs)
+        load_scales(tab_s, tab_scales)
+        wb_raw[0, 0] = load_rows("wb00", wb, 0, 0, KP)
+        tab_w[1] = load_table(1)
+        load_scales(wa_s, wa_scales)
+        wa_w[0] = load_wa(0)
+        wb_raw[0, 1] = load_rows("wb01", wb, KP, 0, KP)
+        wc_raw[0, 0] = [load_rows("wc00", wc, 0, 0, KP)]
+        wc_raw[0, 1] = [load_rows("wc01%d" % s, wc, KP, s * 256, 256) for s in range(2)]
+        gt_sb = held("gt_sb", [P, HALVES, PACK], F32)
+        nc.sync.dma_start(out=gt_sb[:], in_=gt.rearrange("(b p t) -> p b t", b=HALVES, t=PACK))
+        idx2 = load_list("idx2", offs2)
+        wgs_sb = held("wgs_sb", [P, S], F32)
+        nc.sync.dma_start(out=wgs_sb[:], in_=wgs)
+        idx3 = load_list("idx3", offs3)
+        wb_raw[1, 0] = load_rows("wb10", wb, 0, KP, KP)
+        wa_w[1] = load_wa(1)
+        wb_raw[1, 1] = load_rows("wb11", wb, KP, KP, KP)
+        wc_raw[1, 0] = [load_rows("wc10", wc, 0, KP, KP)]
+        wc_raw[1, 1] = [load_rows("wc11", wc, KP, KP, KP)]
+        wu_raw = load_rows("wu_raw", wu, 0, 0, N)
+        wl_w = held("wl_w", [P, 2 * N], U8)
+        nc.sync.dma_start(out=wl_w[:].bitcast(I32), in_=wl_words[0].bitcast(I32))
+        load_scales(wl_s, wl_scales)
+        lay_sb = [load_rows("lay%d" % b, lay, b * KP, 0, M) for b in range(HALVES)]
+
+        v_w, v_s = {}, {}
+
+        def gather_table(a):
+            v_w[a] = held("v_w%d" % a, [P, S], U32)
+            v_s[a] = held("v_s%d" % a, [P, S], U8)
+            nc.vector.tensor_copy(v_w[a][:], tab_w[a][:].indirect(idx[:]))
+            nc.vector.tensor_copy(v_s[a][:], tab_s[:, a, :].indirect(idx[:]))
+
+        def copy_on(engine, dst, src):
+            if engine == "scalar":
+                nc.scalar.copy(out=dst, in_=src)
+            else:
+                nc.vector.tensor_copy(out=dst, in_=src)
+
+        def round_plain(raw, engine):
+            grouped = ring.tile([P, KP, PACK], BF16, name="grouped", align_bytes=64)
+            copy_on(
+                engine,
+                grouped[:].rearrange("p (c i) j -> p c j i", i=4),
+                raw[:].rearrange("p j (c i) -> p c j i", i=4),
+            )
+            return grouped[:].rearrange("p c j -> p (c j)")
+
+        def round_dealt(raws, engines):
+            grouped = ring.tile([P, PACK, P, PACK], BF16, name="grouped", align_bytes=64)
+            share = P // len(raws)
+            for s, (raw, engine) in enumerate(zip(raws, engines)):
+                copy_on(
+                    engine,
+                    grouped[:, :, s * share : (s + 1) * share, :].rearrange("p t q j -> p q j t"),
+                    raw[:].rearrange("p j (q t) -> p q j t", t=PACK),
+                )
+            return grouped[:].rearrange("p t q j -> p (t q j)")
+
+        def quantize(codes, scales, grouped, cuts):
+            for lo, hi in cuts:
+                nc.vector.quantize_mx(
+                    out=codes[:, lo:hi].bitcast(FP8X4),
+                    scales=scales[:, lo:hi],
+                    in_=grouped[:, PACK * lo : PACK * hi],
+                )
+
+        def quantized(name, grouped, width, cuts, tag=None):
+            codes = held(name + "_w", [P, width], U32, tag)
+            scales = held(name + "_s", [P, width], U8)
+            quantize(codes, scales, grouped, cuts)
+            return codes, scales
+
+        whole = [(0, KP)]
+        wb_q, wc_q, max_t = {}, {}, {}
+
+        def product_a(b):
+            a_sb = []
+            for c in range(S // P):
+                cols = slice(c * P, (c + 1) * P)
+                bank = psum.tile([P, KP], F32, name="a_bank", tag="a")
+                for a in range(PASSES):
+                    nc.tensor.matmul_mx(
+                        out=bank[:],
+                        lhsT=v_w[a][:, cols].bitcast(FP8X4), lhsT_scale=v_s[a][:, cols],
+                        rhs=wa_w[b][:, a, :].bitcast(FP4X4), rhs_scale=wa_s[:, a, b * KP : (b + 1) * KP],
+                        start=(a == 0), stop=(a == PASSES - 1),
+                    )
+                a_tile = ring.tile([P, PACK, P], F32, name="a_tile")
+                nc.scalar.copy(out=a_tile[:], in_=bank[:].rearrange("j (q t) -> j t q", t=PACK))
+                a_sb.append(a_tile)
+            return a_sb
+
+        def product_b_and_max(b, a_sb):
+            max_t[b] = held("max_t%d" % b, [P, S // P, PACK, P], F32, ("max_t0", "wb01")[b])
+            for c in range(S // P):
+                cols = slice(c * P, (c + 1) * P)
+                bank = psum.tile([P, KP], F32, name="b_bank", tag="b")
+                for a in range(PASSES):
+                    codes, scales = wb_q[b, a]
+                    nc.tensor.matmul_mx(
+                        out=bank[:],
+                        lhsT=v_w[a][:, cols].bitcast(FP8X4), lhsT_scale=v_s[a][:, cols],
+                        rhs=codes[:].bitcast(FP8X4), rhs_scale=scales[:],
+                        start=(a == 0), stop=(a == PASSES - 1),
+                    )
+                nc.vector.tensor_tensor(
+                    out=max_t[b][:, c], in0=bank[:].rearrange("j (q t) -> j t q", t=PACK), in1=a_sb[c][:],
+                    op=ALU.max,
+                )
+
+        tanh_d, h = {}, {}
+
+        def product_d(i):
+            b, t = divmod(i, PACK)
+            cols = slice(t * P, (t + 1) * P)
+            bank = psum.tile([P, S], F32, name="d_bank", tag="d")
+            for a in range(PASSES):
+                codes, scales = wc_q[b, a]
+                nc.tensor.matmul_mx(
+                    out=bank[:],
+                    lhsT=codes[:, cols].bitcast(FP8X4), lhsT_scale=scales[:, cols],
+                    rhs=v_w[a][:].bitcast(FP8X4), rhs_scale=v_s[a][:],
+                    start=(a == 0), stop=(a == PASSES - 1),
+                )
+            if t == 0:
+                tanh_d[b] = held("tanh_d%d" % b, [P, PACK, S], F32, ("tanh_d0", "wb00")[b])
+            nc.scalar.activation(out=tanh_d[b][:, t, :], in_=bank[:], func=ACT.Tanh)
+
+        def features(i):
+            b, t = divmod(i, PACK)
+            bank = psum.tile([P, S], F32, name="m_bank", tag="m")
+            for c in range(S // P):
+                nc.tensor.transpose(bank[:, c * P : (c + 1) * P], max_t[b][:, c, t, :], ident[:])
+            h[i] = ring.tile([P, S], F32, name="h")
+            nc.vector.scalar_tensor_tensor(
+                out=h[i][:], in0=tanh_d[b][:, t, :], scalar=gt_sb[:, b, t : t + 1], in1=bank[:],
+                op0=ALU.mult, op1=ALU.add,
+            )
+
+        def scatter(i):
+            nc.vector.tensor_tensor(
+                out=pages[i % PAGES][:].indirect(idx2[:]), in0=h[i][:], in1=wgs_sb[:], op=ALU.mult
+            )
+
+        x = [held("x%d" % b, [P, PACK, M], F32, "tab_w%d" % b) for b in range(HALVES)]
+        cos_x = {}
+
+        def pick(i, lo, hi):
+            b, t = divmod(i, PACK)
+            nc.vector.tensor_copy(
+                x[b][:, t, lo:hi], pages[i % PAGES][:].indirect(idx3[:, lo // 16 : hi // 16])
+            )
+
+        def cosine(i, lo, hi):
+            b, t = divmod(i, PACK)
+            part = cos_x[b][:, t, lo:hi]
+            nc.scalar.activation(out=part, in_=x[b][:, t, lo:hi], func=ACT.Abs)
+            nc.scalar.activation(out=part, in_=part, func=ACT.Sin, scale=-1.0, bias=math.pi / 2)
+
+        def make_z(name, b, lo, hi):
+            grouped = ring.tile([P, hi - lo, PACK], BF16, name="grouped", align_bytes=64)
+            nc.vector.tensor_tensor(
+                out=grouped[:].rearrange("p (c i) t -> p c t i", i=4),
+                in0=cos_x[b][:, :, lo:hi].rearrange("p t (c i) -> p c t i", i=4),
+                in1=lay_sb[b][:, :, lo:hi].rearrange("p t (c i) -> p c t i", i=4),
+                op=ALU.mult,
+            )
+            return quantized(name, grouped[:].rearrange("p m t -> p (m t)"), hi - lo, [(0, hi - lo)])
+
+        gather_table(0)
+        grouped_b0 = round_plain(wb_raw[0, 0], "scalar")
+        gather_table(1)
+        wb_q[0, 0] = quantized("wb00", grouped_b0, KP, whole)
+        a_sb = product_a(0)
+        wb_q[0, 1] = quantized("wb01", round_plain(wb_raw[0, 1], "vector"), KP, whole)
+        grouped_c0 = round_dealt(wc_raw[0, 0], ["scalar"])
+        product_b_and_max(0, a_sb)
+        wc_q[0, 0] = quantized("wc00", grouped_c0, KP, whole)
+        wc_q[0, 1] = quantized("wc01", round_dealt(wc_raw[0, 1], ["scalar", "vector"]), KP, [(0, P), (P, KP)])
+        for i in range(PACK):
+            product_d(i)
+        features(0)
+        features(1)
+        scatter(0)
+
+        wb_q[1, 0] = quantized("wb10", round_plain(wb_raw[1, 0], "scalar"), KP, whole)
+        a_sb = product_a(1)
+        features(2)
+        scatter(1)
+        pick(0, 0, M)
+        wb_q[1, 1] = quantized("wb11", round_plain(wb_raw[1, 1], "scalar"), KP, whole)
+        wc_q[1, 0] = quantized("wc10", round_dealt(wc_raw[1, 0], ["scalar"]), KP, whole)
+        features(3)
+        product_b_and_max(1, a_sb)
+        wc_q[1, 1] = quantized("wc11", round_dealt(wc_raw[1, 1], ["scalar"]), KP, whole, tag="late")
+        for i in range(PACK, 2 * PACK):
+            product_d(i)
+        wu_w, wu_s = quantized("wu", round_plain(wu_raw, "scalar"), N, whole)
+        scatter(2)
+        pick(1, 0, M)
+        features(4)
+        scatter(3)
+        pick(2, 0, M)
+        features(5)
+        scatter(4)
+        pick(3, 0, M)
+        cos_x[0] = held("cos0", [P, PACK, M], F32, tag="late")
+        cos_x[1] = x[1]
+        for i in range(PACK):
+            cosine(i, 0, M)
+        features(6)
+        scatter(5)
+        pick(4, 0, M)
+        cosine(4, 0, M)
+        z_up = make_z("z_up", 0, 0, M)
+        features(7)
+        scatter(6)
+        pick(5, 0, M)
+        cosine(5, 0, M)
+        scatter(7)
+        for lo in (0, MH):
+            for i in (6, 7):
+                pick(i, lo, lo + MH)
+                cosine(i, lo, lo + MH)
+
+        banks = {}
+        for s in range(2):
+            for c in range(N // P):
+                tag = ("a", "b", "m", "d")[2 * s + c // 2]
+                banks[s, c] = psum.tile([P, MH], F32, name="y_bank", tag=tag)
+                cols = slice(c * P, (c + 1) * P)
+                nc.tensor.matmul_mx(
+                    out=banks[s, c][:],
+                    lhsT=wu_w[:, cols].bitcast(FP8X4), lhsT_scale=wu_s[:, cols],
+                    rhs=z_up[0][:, s * MH : (s + 1) * MH].bitcast(FP8X4), rhs_scale=z_up[1][:, s * MH : (s + 1) * MH],
+                    start=True, stop=False,
+                )
+        for s in range(2):
+            z_w, z_s = make_z("z_low%d" % s, 1, s * MH, (s + 1) * MH)
+            result = held("result%d" % s, [P, N // P, MH], F32, "wc01%d" % s)
+            for c in range(N // P):
+                cols = slice(c * P, (c + 1) * P)
+                nc.tensor.matmul_mx(
+                    out=banks[s, c][:],
+                    lhsT=wl_w[:, 2 * c * P : 2 * (c + 1) * P].bitcast(FP4X4), lhsT_scale=wl_s[:, 0, cols],
+                    rhs=z_w[:].bitcast(FP8X4), rhs_scale=z_s[:],
+                    start=False, stop=True,
+                )
+                nc.scalar.activation(out=result[:, c, :], in_=banks[s, c][:], func=ACT.Gelu_apprx_tanh)
+                nc.sync.dma_start(out=out[cols, s * MH : (s + 1) * MH], in_=result[:, c, :])

@@ -23,8 +23,9 @@ PACK = 4
 KP = P * PACK
 PASSES = K // KP
 HALVES = H // KP
-PAGES = 4
+PAGES = 3
 MH = M // 2
+H_TAGS = {2: "tanh1", 3: "wc01_w"}
 
 
 def tile_list_portal_tag_motion_kernel(
@@ -34,7 +35,7 @@ def tile_list_portal_tag_motion_kernel(
     nc = tc.nc
     with ExitStack() as ctx:
         keep = ctx.enter_context(tc.tile_pool(name="keep", bufs=1))
-        ring = ctx.enter_context(tc.tile_pool(name="ring", bufs=4))
+        ring = ctx.enter_context(tc.tile_pool(name="ring", bufs=3))
         psum = ctx.enter_context(tc.psum_pool(name="psum", bufs=2))
 
         def held(name, shape, dtype, tag=None):
@@ -48,7 +49,7 @@ def tile_list_portal_tag_motion_kernel(
         nc.gpsimd.memset(wl_s[:].bitcast(I32), 0)
         pages = [held("page%d" % i, [P, T2], F32) for i in range(PAGES)]
         for page in pages:
-            nc.vector.memset(page[:], 0.0)
+            nc.gpsimd.memset(page[:], 0.0)
 
         ident = held("ident", [P, P], F32)
         make_identity(nc, ident[:])
@@ -92,12 +93,12 @@ def tile_list_portal_tag_motion_kernel(
         tab_w[0] = load_table(0)
         idx = load_list("idx", offs)
         load_scales(tab_s, tab_scales)
-        wb_raw[0, 0] = load_rows("wb00", wb, 0, 0, KP)
         tab_w[1] = load_table(1)
-        load_scales(wa_s, wa_scales)
         wa_w[0] = load_wa(0)
-        wb_raw[0, 1] = load_rows("wb01", wb, KP, 0, KP)
-        wc_raw[0, 0] = [load_rows("wc00", wc, 0, 0, KP)]
+        load_scales(wa_s, wa_scales)
+        wb_raw[0, 0] = [load_rows("wb00", wb, 0, 0, KP)]
+        wb_raw[0, 1] = [load_rows("wb01%d" % s, wb, KP, s * 256, 256) for s in range(2)]
+        wc_raw[0, 0] = [load_rows("wc00%d" % s, wc, 0, s * 256, 256) for s in range(2)]
         wc_raw[0, 1] = [load_rows("wc01%d" % s, wc, KP, s * 256, 256) for s in range(2)]
         gt_sb = held("gt_sb", [P, HALVES, PACK], F32)
         nc.sync.dma_start(out=gt_sb[:], in_=gt.rearrange("(b p t) -> p b t", b=HALVES, t=PACK))
@@ -105,12 +106,12 @@ def tile_list_portal_tag_motion_kernel(
         wgs_sb = held("wgs_sb", [P, S], F32)
         nc.sync.dma_start(out=wgs_sb[:], in_=wgs)
         idx3 = load_list("idx3", offs3)
-        wb_raw[1, 0] = load_rows("wb10", wb, 0, KP, KP)
+        wb_raw[1, 0] = [load_rows("wb10", wb, 0, KP, KP)]
         wa_w[1] = load_wa(1)
-        wb_raw[1, 1] = load_rows("wb11", wb, KP, KP, KP)
+        wb_raw[1, 1] = [load_rows("wb11", wb, KP, KP, KP)]
         wc_raw[1, 0] = [load_rows("wc10", wc, 0, KP, KP)]
         wc_raw[1, 1] = [load_rows("wc11", wc, KP, KP, KP)]
-        wu_raw = load_rows("wu_raw", wu, 0, 0, N)
+        wu_raw = [load_rows("wu_raw", wu, 0, 0, N)]
         wl_w = held("wl_w", [P, 2 * N], U8)
         nc.sync.dma_start(out=wl_w[:].bitcast(I32), in_=wl_words[0].bitcast(I32))
         load_scales(wl_s, wl_scales)
@@ -121,8 +122,11 @@ def tile_list_portal_tag_motion_kernel(
         def gather_table(a):
             v_w[a] = held("v_w%d" % a, [P, S], U32)
             v_s[a] = held("v_s%d" % a, [P, S], U8)
-            nc.vector.tensor_copy(v_w[a][:], tab_w[a][:].indirect(idx[:]))
+            if a == 0:
+                nc.vector.tensor_copy(v_w[a][:], tab_w[a][:].indirect(idx[:]))
             nc.vector.tensor_copy(v_s[a][:], tab_s[:, a, :].indirect(idx[:]))
+            if a == 1:
+                nc.vector.tensor_copy(v_w[a][:], tab_w[a][:].indirect(idx[:]))
 
         def copy_on(engine, dst, src):
             if engine == "scalar":
@@ -130,17 +134,19 @@ def tile_list_portal_tag_motion_kernel(
             else:
                 nc.vector.tensor_copy(out=dst, in_=src)
 
-        def round_plain(raw, engine):
-            grouped = ring.tile([P, KP, PACK], BF16, name="grouped", align_bytes=64)
-            copy_on(
-                engine,
-                grouped[:].rearrange("p (c i) j -> p c j i", i=4),
-                raw[:].rearrange("p j (c i) -> p c j i", i=4),
-            )
+        def round_plain(raws, engines, tag):
+            grouped = held("grouped", [P, KP, PACK], BF16, tag)
+            share = KP // len(raws)
+            for s, (raw, engine) in enumerate(zip(raws, engines)):
+                copy_on(
+                    engine,
+                    grouped[:, s * share : (s + 1) * share, :].rearrange("p (c i) j -> p c j i", i=4),
+                    raw[:].rearrange("p j (c i) -> p c j i", i=4),
+                )
             return grouped[:].rearrange("p c j -> p (c j)")
 
-        def round_dealt(raws, engines):
-            grouped = ring.tile([P, PACK, P, PACK], BF16, name="grouped", align_bytes=64)
+        def round_dealt(raws, engines, tag):
+            grouped = held("grouped", [P, PACK, P, PACK], BF16, tag)
             share = P // len(raws)
             for s, (raw, engine) in enumerate(zip(raws, engines)):
                 copy_on(
@@ -167,40 +173,37 @@ def tile_list_portal_tag_motion_kernel(
         whole = [(0, KP)]
         wb_q, wc_q, max_t = {}, {}, {}
 
-        def product_a(b):
-            a_sb = []
-            for c in range(S // P):
-                cols = slice(c * P, (c + 1) * P)
-                bank = psum.tile([P, KP], F32, name="a_bank", tag="a")
-                for a in range(PASSES):
+        def by_entries(tags, moving, chunks):
+            banks = {c: psum.tile([P, KP], F32, name="t_bank", tag=tags[c // 2]) for c in chunks}
+            for a in range(PASSES):
+                rhs, rhs_scale = moving[a]
+                for c in chunks:
+                    cols = slice(c * P, (c + 1) * P)
                     nc.tensor.matmul_mx(
-                        out=bank[:],
+                        out=banks[c][:],
                         lhsT=v_w[a][:, cols].bitcast(FP8X4), lhsT_scale=v_s[a][:, cols],
-                        rhs=wa_w[b][:, a, :].bitcast(FP4X4), rhs_scale=wa_s[:, a, b * KP : (b + 1) * KP],
+                        rhs=rhs, rhs_scale=rhs_scale,
                         start=(a == 0), stop=(a == PASSES - 1),
                     )
-                a_tile = ring.tile([P, PACK, P], F32, name="a_tile")
-                nc.scalar.copy(out=a_tile[:], in_=bank[:].rearrange("j (q t) -> j t q", t=PACK))
-                a_sb.append(a_tile)
+            return [(c, banks[c][:].rearrange("j (q t) -> j t q", t=PACK)) for c in chunks]
+
+        def product_a(b, tags, runs):
+            moving = [
+                (wa_w[b][:, a, :].bitcast(FP4X4), wa_s[:, a, b * KP : (b + 1) * KP]) for a in range(PASSES)
+            ]
+            a_sb = []
+            for chunks in runs:
+                for c, bank in by_entries(tags, moving, chunks):
+                    a_tile = held("a%d%d" % (b, c), [P, PACK, P], F32)
+                    nc.scalar.copy(out=a_tile[:], in_=bank)
+                    a_sb.append(a_tile)
             return a_sb
 
-        def product_b_and_max(b, a_sb):
-            max_t[b] = held("max_t%d" % b, [P, S // P, PACK, P], F32, ("max_t0", "wb01")[b])
-            for c in range(S // P):
-                cols = slice(c * P, (c + 1) * P)
-                bank = psum.tile([P, KP], F32, name="b_bank", tag="b")
-                for a in range(PASSES):
-                    codes, scales = wb_q[b, a]
-                    nc.tensor.matmul_mx(
-                        out=bank[:],
-                        lhsT=v_w[a][:, cols].bitcast(FP8X4), lhsT_scale=v_s[a][:, cols],
-                        rhs=codes[:].bitcast(FP8X4), rhs_scale=scales[:],
-                        start=(a == 0), stop=(a == PASSES - 1),
-                    )
-                nc.vector.tensor_tensor(
-                    out=max_t[b][:, c], in0=bank[:].rearrange("j (q t) -> j t q", t=PACK), in1=a_sb[c][:],
-                    op=ALU.max,
-                )
+        def product_b_and_max(b, a_sb, tags):
+            max_t[b] = held("max_t%d" % b, [P, S // P, PACK, P], F32, ("max_t0", "wb00")[b])
+            moving = [(wb_q[b, a][0][:].bitcast(FP8X4), wb_q[b, a][1][:]) for a in range(PASSES)]
+            for c, bank in by_entries(tags, moving, range(S // P)):
+                nc.vector.tensor_tensor(out=max_t[b][:, c], in0=bank, in1=a_sb[c][:], op=ALU.max)
 
         tanh_d, h = {}, {}
 
@@ -216,18 +219,20 @@ def tile_list_portal_tag_motion_kernel(
                     rhs=v_w[a][:].bitcast(FP8X4), rhs_scale=v_s[a][:],
                     start=(a == 0), stop=(a == PASSES - 1),
                 )
-            if t == 0:
-                tanh_d[b] = held("tanh_d%d" % b, [P, PACK, S], F32, ("tanh_d0", "wb00")[b])
-            nc.scalar.activation(out=tanh_d[b][:, t, :], in_=bank[:], func=ACT.Tanh)
+            tanh_d[i] = held("tanh_d%d" % i, [P, S], F32, ("tanh0", "tanh1", "tanh2", "tanh3", "wb010", "wb011", "wc000", "wc001")[i])
+            nc.scalar.activation(out=tanh_d[i][:], in_=bank[:], func=ACT.Tanh)
 
         def features(i):
             b, t = divmod(i, PACK)
             bank = psum.tile([P, S], F32, name="m_bank", tag="m")
             for c in range(S // P):
                 nc.tensor.transpose(bank[:, c * P : (c + 1) * P], max_t[b][:, c, t, :], ident[:])
-            h[i] = ring.tile([P, S], F32, name="h")
+            if i in H_TAGS:
+                h[i] = held("h", [P, S], F32, H_TAGS[i])
+            else:
+                h[i] = ring.tile([P, S], F32, name="h")
             nc.vector.scalar_tensor_tensor(
-                out=h[i][:], in0=tanh_d[b][:, t, :], scalar=gt_sb[:, b, t : t + 1], in1=bank[:],
+                out=h[i][:], in0=tanh_d[i][:], scalar=gt_sb[:, b, t : t + 1], in1=bank[:],
                 op0=ALU.mult, op1=ALU.add,
             )
 
@@ -236,7 +241,7 @@ def tile_list_portal_tag_motion_kernel(
                 out=pages[i % PAGES][:].indirect(idx2[:]), in0=h[i][:], in1=wgs_sb[:], op=ALU.mult
             )
 
-        x = [held("x%d" % b, [P, PACK, M], F32, "tab_w%d" % b) for b in range(HALVES)]
+        x = {}
         cos_x = {}
 
         def pick(i, lo, hi):
@@ -251,8 +256,8 @@ def tile_list_portal_tag_motion_kernel(
             nc.scalar.activation(out=part, in_=x[b][:, t, lo:hi], func=ACT.Abs)
             nc.scalar.activation(out=part, in_=part, func=ACT.Sin, scale=-1.0, bias=math.pi / 2)
 
-        def make_z(name, b, lo, hi):
-            grouped = ring.tile([P, hi - lo, PACK], BF16, name="grouped", align_bytes=64)
+        def make_z(name, b, lo, hi, tag):
+            grouped = held("grouped", [P, hi - lo, PACK], BF16, tag)
             nc.vector.tensor_tensor(
                 out=grouped[:].rearrange("p (c i) t -> p c t i", i=4),
                 in0=cos_x[b][:, :, lo:hi].rearrange("p t (c i) -> p c t i", i=4),
@@ -262,39 +267,44 @@ def tile_list_portal_tag_motion_kernel(
             return quantized(name, grouped[:].rearrange("p m t -> p (m t)"), hi - lo, [(0, hi - lo)])
 
         gather_table(0)
-        grouped_b0 = round_plain(wb_raw[0, 0], "scalar")
         gather_table(1)
-        wb_q[0, 0] = quantized("wb00", grouped_b0, KP, whole)
-        a_sb = product_a(0)
-        wb_q[0, 1] = quantized("wb01", round_plain(wb_raw[0, 1], "vector"), KP, whole)
-        grouped_c0 = round_dealt(wc_raw[0, 0], ["scalar"])
-        product_b_and_max(0, a_sb)
-        wc_q[0, 0] = quantized("wc00", grouped_c0, KP, whole)
-        wc_q[0, 1] = quantized("wc01", round_dealt(wc_raw[0, 1], ["scalar", "vector"]), KP, [(0, P), (P, KP)])
+        a_sb = product_a(0, ("a", "d"), [range(4)])
+        wb_q[0, 0] = quantized("wb00", round_plain(wb_raw[0, 0], ["vector"], "tab_w1"), KP, whole)
+        wb_q[0, 1] = quantized("wb01", round_plain(wb_raw[0, 1], ["vector", "vector"], "tab_w0"), KP, whole)
+        grouped_c0 = round_dealt(wc_raw[0, 0], ["scalar", "scalar"], "wa_w0")
+        product_b_and_max(0, a_sb, ("b", "m"))
+        wc_q[0, 0] = quantized("wc00", grouped_c0, KP, whole, tag="a01")
+        wc_q[0, 1] = quantized("wc01", round_dealt(wc_raw[0, 1], ["scalar", "scalar"], "wc001"), KP, [(0, P), (P, KP)])
         for i in range(PACK):
             product_d(i)
+        for b in range(HALVES):
+            x[b] = held("x%d" % b, [P, PACK, M], F32, "tab_w%d" % b)
         features(0)
         features(1)
         scatter(0)
 
-        wb_q[1, 0] = quantized("wb10", round_plain(wb_raw[1, 0], "scalar"), KP, whole)
-        a_sb = product_a(1)
-        features(2)
+        grouped_b0 = round_plain(wb_raw[1, 0], ["scalar"], "tanh0")
+        a_sb = product_a(1, ("d", "d"), [[0], [1], [2], [3]])
+        grouped_b1 = round_plain(wb_raw[1, 1], ["scalar"], "tanh1")
+        grouped_c0 = round_dealt(wc_raw[1, 0], ["scalar"], "a01")
+        grouped_c1 = round_dealt(wc_raw[1, 1], ["scalar"], "wc01_w")
         scatter(1)
         pick(0, 0, M)
-        wb_q[1, 1] = quantized("wb11", round_plain(wb_raw[1, 1], "scalar"), KP, whole)
-        wc_q[1, 0] = quantized("wc10", round_dealt(wc_raw[1, 0], ["scalar"]), KP, whole)
+        wb_q[1, 0] = quantized("wb10", grouped_b0, KP, whole)
+        wb_q[1, 1] = quantized("wb11", grouped_b1, KP, whole)
+        features(2)
+        scatter(2)
+        product_b_and_max(1, a_sb, ("b", "a"))
+        wc_q[1, 0] = quantized("wc10", grouped_c0, KP, whole)
+        wc_q[1, 1] = quantized("wc11", grouped_c1, KP, whole, tag="late")
         features(3)
-        product_b_and_max(1, a_sb)
-        wc_q[1, 1] = quantized("wc11", round_dealt(wc_raw[1, 1], ["scalar"]), KP, whole, tag="late")
         for i in range(PACK, 2 * PACK):
             product_d(i)
-        wu_w, wu_s = quantized("wu", round_plain(wu_raw, "scalar"), N, whole)
-        scatter(2)
+        wu_w, wu_s = quantized("wu", round_plain(wu_raw, ["scalar"], "tanh0"), N, whole)
         pick(1, 0, M)
-        features(4)
         scatter(3)
         pick(2, 0, M)
+        features(4)
         features(5)
         scatter(4)
         pick(3, 0, M)
@@ -306,7 +316,7 @@ def tile_list_portal_tag_motion_kernel(
         scatter(5)
         pick(4, 0, M)
         cosine(4, 0, M)
-        z_up = make_z("z_up", 0, 0, M)
+        z_up = make_z("z_up", 0, 0, M, "wb10")
         features(7)
         scatter(6)
         pick(5, 0, M)
@@ -330,7 +340,7 @@ def tile_list_portal_tag_motion_kernel(
                     start=True, stop=False,
                 )
         for s in range(2):
-            z_w, z_s = make_z("z_low%d" % s, 1, s * MH, (s + 1) * MH)
+            z_w, z_s = make_z("z_low%d" % s, 1, s * MH, (s + 1) * MH, ("wb11", "wc10")[s])
             result = held("result%d" % s, [P, N // P, MH], F32, "wc01%d" % s)
             for c in range(N // P):
                 cols = slice(c * P, (c + 1) * P)

@@ -45,20 +45,20 @@ def tile_list_portal_tag_motion_kernel(
         wa_s = held("wa_s", [P, PASSES, H], U8)
         wl_s = held("wl_s", [P, 1, N], U8)
         nc.vector.memset(tab_s[:].bitcast(I32), 0)
-        nc.gpsimd.memset(wa_s[:].bitcast(I32), 0)
-        nc.gpsimd.memset(wl_s[:].bitcast(I32), 0)
+        nc.vector.memset(wa_s[:].bitcast(I32), 0)
+        nc.vector.memset(wl_s[:].bitcast(I32), 0)
         pages = [held("page%d" % i, [P, T2], F32) for i in range(PAGES)]
         for page in pages:
-            nc.gpsimd.memset(page[:], 0.0)
+            nc.vector.memset(page[:], 0.0)
 
         ident = held("ident", [P, P], F32)
         make_identity(nc, ident[:])
 
         def load_scales(plane, src):
-            for q in range(4):
+            for r in range(4):
                 nc.sync.dma_start(
-                    out=plane[32 * q : 32 * q + 4].bitcast(I32),
-                    in_=src[:, 4 * q : 4 * q + 4, :].rearrange("a r c -> r a c").bitcast(I32),
+                    out=plane[r:P:32].bitcast(I32),
+                    in_=src[:, r:16:4, :].rearrange("a q c -> q a c").bitcast(I32),
                 )
 
         def load_table(a):
@@ -312,11 +312,14 @@ def tile_list_portal_tag_motion_kernel(
         cos_x[1] = x[1]
         for i in range(PACK):
             cosine(i, 0, M)
+            nc.gpsimd.tensor_tensor(
+                out=cos_x[0][:, i, :], in0=cos_x[0][:, i, :], in1=lay_sb[0][:, i, :], op=ALU.mult
+            )
         features(6)
         scatter(5)
         pick(4, 0, M)
         cosine(4, 0, M)
-        z_up = make_z("z_up", 0, 0, M, "wb10")
+        z_up = quantized("z_up", round_plain([cos_x[0]], ["scalar"], "wb10"), M, whole)
         features(7)
         scatter(6)
         pick(5, 0, M)

import math
from contextlib import ExitStack

import concourse.mybir as mybir
from concourse.masks import make_identity

K, T, S, H, HU, T2, M, N = 1024, 2048, 512, 1024, 512, 1024, 512, 512
FLOPS = 2 * 3 * K * H * S + 2 * H * N * M

F32 = mybir.dt.float32
BF16 = mybir.dt.bfloat16
I32 = mybir.dt.int32
U32 = mybir.dt.uint32
U16 = mybir.dt.uint16
U8 = mybir.dt.uint8
FP8X4 = mybir.dt.float8_e4m3fn_x4
FP4X4 = mybir.dt.float4_e2m1fn_x4
ALU = mybir.AluOpType
ACT = mybir.ActivationFunctionType

P = 128
PACK = 4
KP = P * PACK
PASSES = K // KP
HALVES = H // KP
PAGES = 3
MH = M // 2
H_TAGS = {2: "tanh1", 3: "wc01_w"}


def tile_list_portal_tag_motion_kernel(
    tc, tab_words, tab_scales, offs, offs2, offs3, wa_words, wa_scales, wb, wc, gt, wgs, lay, wu,
    wl_words, wl_scales, out,
):
    nc = tc.nc
    with ExitStack() as ctx:
        keep = ctx.enter_context(tc.tile_pool(name="keep", bufs=1))
        ring = ctx.enter_context(tc.tile_pool(name="ring", bufs=3))
        psum = ctx.enter_context(tc.psum_pool(name="psum", bufs=2))

        def held(name, shape, dtype, tag=None):
            return keep.tile(shape, dtype, name=name, tag=tag or name, align_bytes=64)

        tab_s = held("tab_s", [P, PASSES, T], U8)
        wa_s = held("wa_s", [P, PASSES, H], U8)
        wl_s = held("wl_s", [P, 1, N], U8)
        nc.vector.memset(tab_s[:].bitcast(I32), 0)
        nc.vector.memset(wa_s[:].bitcast(I32), 0)
        nc.vector.memset(wl_s[:].bitcast(I32), 0)
        pages = [held("page%d" % i, [P, T2], F32) for i in range(PAGES)]
        for page in pages:
            nc.vector.memset(page[:], 0.0)

        ident = held("ident", [P, P], F32)
        make_identity(nc, ident[:])

        def load_scales(plane, src):
            for r in range(4):
                nc.sync.dma_start(
                    out=plane[r:P:32].bitcast(I32),
                    in_=src[:, r:16:4, :].rearrange("a q c -> q a c").bitcast(I32),
                )

        def load_table(a):
            words = held("tab_w%d" % a, [P, T], U32)
            nc.sync.dma_start(
                out=words[:].bitcast(I32), in_=tab_words[a].rearrange("p t i -> p (t i)").bitcast(I32)
            )
            return words

        def load_list(name, src):
            lst = keep.tile([P, S // 16], U16, name=name)
            nc.sync.dma_start(lst[:], src)
            return lst

        def load_rows(name, src, row0, col0, width):
            raw = held(name, [P, PACK, width], F32)
            nc.sync.dma_start(
                out=raw[:],
                in_=src[row0 : row0 + KP, col0 : col0 + width].rearrange("(p j) c -> p j c", j=PACK),
            )
            return raw

        def load_wa(b):
            words = held("wa_w%d" % b, [P, PASSES, 2 * KP], U8)
            nc.sync.dma_start(
                out=words[:].bitcast(I32),
                in_=wa_words[:, :, 2 * KP * b : 2 * KP * (b + 1)].rearrange("a p c -> p a c").bitcast(I32),
            )
            return words

        tab_w, wa_w, wb_raw, wc_raw = {}, {}, {}, {}
        tab_w[0] = load_table(0)
        idx = load_list("idx", offs)
        load_scales(tab_s, tab_scales)
        tab_w[1] = load_table(1)
        wa_w[0] = load_wa(0)
        load_scales(wa_s, wa_scales)
        wb_raw[0, 0] = [load_rows("wb00", wb, 0, 0, KP)]
        wb_raw[0, 1] = [load_rows("wb01%d" % s, wb, KP, s * 256, 256) for s in range(2)]
        wc_raw[0, 0] = [load_rows("wc00%d" % s, wc, 0, s * 256, 256) for s in range(2)]
        wc_raw[0, 1] = [load_rows("wc01%d" % s, wc, KP, s * 256, 256) for s in range(2)]
        gt_sb = held("gt_sb", [P, HALVES, PACK], F32)
        nc.sync.dma_start(out=gt_sb[:], in_=gt.rearrange("(b p t) -> p b t", b=HALVES, t=PACK))
        idx2 = load_list("idx2", offs2)
        wgs_sb = held("wgs_sb", [P, S], F32)
        nc.sync.dma_start(out=wgs_sb[:], in_=wgs)
        idx3 = load_list("idx3", offs3)
        wb_raw[1, 0] = [load_rows("wb10", wb, 0, KP, KP)]
        wa_w[1] = load_wa(1)
        wb_raw[1, 1] = [load_rows("wb11", wb, KP, KP, KP)]
        wc_raw[1, 0] = [load_rows("wc10", wc, 0, KP, KP)]
        wc_raw[1, 1] = [load_rows("wc11", wc, KP, KP, KP)]
        wu_raw = [load_rows("wu_raw", wu, 0, 0, N)]
        wl_w = held("wl_w", [P, 2 * N], U8)
        nc.sync.dma_start(out=wl_w[:].bitcast(I32), in_=wl_words[0].bitcast(I32))
        load_scales(wl_s, wl_scales)
        lay_sb = [load_rows("lay%d" % b, lay, b * KP, 0, M) for b in range(HALVES)]

        v_w, v_s = {}, {}

        def gather_table(a):
            v_w[a] = held("v_w%d" % a, [P, S], U32)
            v_s[a] = held("v_s%d" % a, [P, S], U8)
            if a == 0:
                nc.vector.tensor_copy(v_w[a][:], tab_w[a][:].indirect(idx[:]))
            nc.vector.tensor_copy(v_s[a][:], tab_s[:, a, :].indirect(idx[:]))
            if a == 1:
                nc.vector.tensor_copy(v_w[a][:], tab_w[a][:].indirect(idx[:]))

        def copy_on(engine, dst, src):
            if engine == "scalar":
                nc.scalar.copy(out=dst, in_=src)
            else:
                nc.vector.tensor_copy(out=dst, in_=src)

        def round_plain(raws, engines, tag):
            grouped = held("grouped", [P, KP, PACK], BF16, tag)
            share = KP // len(raws)
            for s, (raw, engine) in enumerate(zip(raws, engines)):
                copy_on(
                    engine,
                    grouped[:, s * share : (s + 1) * share, :].rearrange("p (c i) j -> p c j i", i=4),
                    raw[:].rearrange("p j (c i) -> p c j i", i=4),
                )
            return grouped[:].rearrange("p c j -> p (c j)")

        def round_dealt(raws, engines, tag):
            grouped = held("grouped", [P, PACK, P, PACK], BF16, tag)
            share = P // len(raws)
            for s, (raw, engine) in enumerate(zip(raws, engines)):
                copy_on(
                    engine,
                    grouped[:, :, s * share : (s + 1) * share, :].rearrange("p t q j -> p q j t"),
                    raw[:].rearrange("p j (q t) -> p q j t", t=PACK),
                )
            return grouped[:].rearrange("p t q j -> p (t q j)")

        def quantize(codes, scales, grouped, cuts):
            for lo, hi in cuts:
                nc.vector.quantize_mx(
                    out=codes[:, lo:hi].bitcast(FP8X4),
                    scales=scales[:, lo:hi],
                    in_=grouped[:, PACK * lo : PACK * hi],
                )

        def quantized(name, grouped, width, cuts, tag=None):
            codes = held(name + "_w", [P, width], U32, tag)
            scales = held(name + "_s", [P, width], U8)
            quantize(codes, scales, grouped, cuts)
            return codes, scales

        whole = [(0, KP)]
        wb_q, wc_q, max_t = {}, {}, {}

        def by_entries(tags, moving, chunks):
            banks = {c: psum.tile([P, KP], F32, name="t_bank", tag=tags[c // 2]) for c in chunks}
            for a in range(PASSES):
                rhs, rhs_scale = moving[a]
                for c in chunks:
                    cols = slice(c * P, (c + 1) * P)
                    nc.tensor.matmul_mx(
                        out=banks[c][:],
                        lhsT=v_w[a][:, cols].bitcast(FP8X4), lhsT_scale=v_s[a][:, cols],
                        rhs=rhs, rhs_scale=rhs_scale,
                        start=(a == 0), stop=(a == PASSES - 1),
                    )
            return [(c, banks[c][:].rearrange("j (q t) -> j t q", t=PACK)) for c in chunks]

        def product_a(b, tags, runs):
            moving = [
                (wa_w[b][:, a, :].bitcast(FP4X4), wa_s[:, a, b * KP : (b + 1) * KP]) for a in range(PASSES)
            ]
            a_sb = []
            for chunks in runs:
                for c, bank in by_entries(tags, moving, chunks):
                    a_tile = held("a%d%d" % (b, c), [P, PACK, P], F32)
                    nc.scalar.copy(out=a_tile[:], in_=bank)
                    a_sb.append(a_tile)
            return a_sb

        def product_b_and_max(b, a_sb, tags):
            max_t[b] = held("max_t%d" % b, [P, S // P, PACK, P], F32, ("max_t0", "wb00")[b])
            moving = [(wb_q[b, a][0][:].bitcast(FP8X4), wb_q[b, a][1][:]) for a in range(PASSES)]
            for c, bank in by_entries(tags, moving, range(S // P)):
                nc.vector.tensor_tensor(out=max_t[b][:, c], in0=bank, in1=a_sb[c][:], op=ALU.max)

        tanh_d, h = {}, {}

        def product_d(i):
            b, t = divmod(i, PACK)
            cols = slice(t * P, (t + 1) * P)
            bank = psum.tile([P, S], F32, name="d_bank", tag="d")
            for a in range(PASSES):
                codes, scales = wc_q[b, a]
                nc.tensor.matmul_mx(
                    out=bank[:],
                    lhsT=codes[:, cols].bitcast(FP8X4), lhsT_scale=scales[:, cols],
                    rhs=v_w[a][:].bitcast(FP8X4), rhs_scale=v_s[a][:],
                    start=(a == 0), stop=(a == PASSES - 1),
                )
            tanh_d[i] = held("tanh_d%d" % i, [P, S], F32, ("tanh0", "tanh1", "tanh2", "tanh3", "wb010", "wb011", "wc000", "wc001")[i])
            nc.scalar.activation(out=tanh_d[i][:], in_=bank[:], func=ACT.Tanh)

        def features(i):
            b, t = divmod(i, PACK)
            bank = psum.tile([P, S], F32, name="m_bank", tag="m")
            for c in range(S // P):
                nc.tensor.transpose(bank[:, c * P : (c + 1) * P], max_t[b][:, c, t, :], ident[:])
            if i in H_TAGS:
                h[i] = held("h", [P, S], F32, H_TAGS[i])
            else:
                h[i] = ring.tile([P, S], F32, name="h")
            nc.vector.scalar_tensor_tensor(
                out=h[i][:], in0=tanh_d[i][:], scalar=gt_sb[:, b, t : t + 1], in1=bank[:],
                op0=ALU.mult, op1=ALU.add,
            )

        def scatter(i):
            nc.vector.tensor_tensor(
                out=pages[i % PAGES][:].indirect(idx2[:]), in0=h[i][:], in1=wgs_sb[:], op=ALU.mult
            )

        x = {}
        cos_x = {}

        def pick(i, lo, hi):
            b, t = divmod(i, PACK)
            nc.vector.tensor_copy(
                x[b][:, t, lo:hi], pages[i % PAGES][:].indirect(idx3[:, lo // 16 : hi // 16])
            )

        def cosine(i, lo, hi):
            b, t = divmod(i, PACK)
            part = cos_x[b][:, t, lo:hi]
            nc.scalar.activation(out=part, in_=x[b][:, t, lo:hi], func=ACT.Abs)
            nc.scalar.activation(out=part, in_=part, func=ACT.Sin, scale=-1.0, bias=math.pi / 2)

        def make_z(name, b, lo, hi, tag):
            grouped = held("grouped", [P, hi - lo, PACK], BF16, tag)
            nc.vector.tensor_tensor(
                out=grouped[:].rearrange("p (c i) t -> p c t i", i=4),
                in0=cos_x[b][:, :, lo:hi].rearrange("p t (c i) -> p c t i", i=4),
                in1=lay_sb[b][:, :, lo:hi].rearrange("p t (c i) -> p c t i", i=4),
                op=ALU.mult,
            )
            return quantized(name, grouped[:].rearrange("p m t -> p (m t)"), hi - lo, [(0, hi - lo)])

        gather_table(0)
        gather_table(1)
        a_sb = product_a(0, ("a", "d"), [range(4)])
        wb_q[0, 0] = quantized("wb00", round_plain(wb_raw[0, 0], ["vector"], "tab_w1"), KP, whole)
        wb_q[0, 1] = quantized("wb01", round_plain(wb_raw[0, 1], ["vector", "vector"], "tab_w0"), KP, whole)
        grouped_c0 = round_dealt(wc_raw[0, 0], ["scalar", "scalar"], "wa_w0")
        product_b_and_max(0, a_sb, ("b", "m"))
        wc_q[0, 0] = quantized("wc00", grouped_c0, KP, whole, tag="a01")
        wc_q[0, 1] = quantized("wc01", round_dealt(wc_raw[0, 1], ["scalar", "scalar"], "wc001"), KP, [(0, P), (P, KP)])
        for i in range(PACK):
            product_d(i)
        for b in range(HALVES):
            x[b] = held("x%d" % b, [P, PACK, M], F32, "tab_w%d" % b)
        features(0)
        features(1)
        scatter(0)

        grouped_b0 = round_plain(wb_raw[1, 0], ["scalar"], "tanh0")
        a_sb = product_a(1, ("d", "d"), [[0], [1], [2], [3]])
        grouped_b1 = round_plain(wb_raw[1, 1], ["scalar"], "tanh1")
        grouped_c0 = round_dealt(wc_raw[1, 0], ["scalar"], "a01")
        grouped_c1 = round_dealt(wc_raw[1, 1], ["scalar"], "wc01_w")
        scatter(1)
        pick(0, 0, M)
        wb_q[1, 0] = quantized("wb10", grouped_b0, KP, whole)
        wb_q[1, 1] = quantized("wb11", grouped_b1, KP, whole)
        features(2)
        scatter(2)
        product_b_and_max(1, a_sb, ("b", "a"))
        wc_q[1, 0] = quantized("wc10", grouped_c0, KP, whole)
        wc_q[1, 1] = quantized("wc11", grouped_c1, KP, whole, tag="late")
        features(3)
        for i in range(PACK, 2 * PACK):
            product_d(i)
        wu_w, wu_s = quantized("wu", round_plain(wu_raw, ["scalar"], "tanh0"), N, whole)
        pick(1, 0, M)
        scatter(3)
        pick(2, 0, M)
        features(4)
        features(5)
        scatter(4)
        pick(3, 0, M)
        cos_x[0] = held("cos0", [P, PACK, M], F32, tag="late")
        cos_x[1] = x[1]
        for i in range(PACK):
            cosine(i, 0, M)
            nc.gpsimd.tensor_tensor(
                out=cos_x[0][:, i, :], in0=cos_x[0][:, i, :], in1=lay_sb[0][:, i, :], op=ALU.mult
            )
        features(6)
        scatter(5)
        pick(4, 0, M)
        cosine(4, 0, M)
        z_up = quantized("z_up", round_plain([cos_x[0]], ["scalar"], "wb10"), M, whole)
        features(7)
        scatter(6)
        pick(5, 0, M)
        cosine(5, 0, M)
        scatter(7)
        for lo in (0, MH):
            for i in (6, 7):
                pick(i, lo, lo + MH)
                cosine(i, lo, lo + MH)

        banks = {}
        for s in range(2):
            for c in range(N // P):
                tag = ("a", "b", "m", "d")[2 * s + c // 2]
                banks[s, c] = psum.tile([P, MH], F32, name="y_bank", tag=tag)
                cols = slice(c * P, (c + 1) * P)
                nc.tensor.matmul_mx(
                    out=banks[s, c][:],
                    lhsT=wu_w[:, cols].bitcast(FP8X4), lhsT_scale=wu_s[:, cols],
                    rhs=z_up[0][:, s * MH : (s + 1) * MH].bitcast(FP8X4), rhs_scale=z_up[1][:, s * MH : (s + 1) * MH],
                    start=True, stop=False,
                )
        for s in range(2):
            z_w, z_s = make_z("z_low%d" % s, 1, s * MH, (s + 1) * MH, ("wb11", "wc10")[s])
            result = held("result%d" % s, [P, N // P, MH], F32, "wc01%d" % s)
            for c in range(N // P):
                cols = slice(c * P, (c + 1) * P)
                nc.tensor.matmul_mx(
                    out=banks[s, c][:],
                    lhsT=wl_w[:, 2 * c * P : 2 * (c + 1) * P].bitcast(FP4X4), lhsT_scale=wl_s[:, 0, cols],
                    rhs=z_w[:].bitcast(FP8X4), rhs_scale=z_s[:],
                    start=False, stop=True,
                )
                nc.scalar.activation(out=result[:, c, :], in_=banks[s, c][:], func=ACT.Gelu_apprx_tanh)
                nc.sync.dma_start(out=out[cols, s * MH : (s + 1) * MH], in_=result[:, c, :])
